import numpy as np
import ml_dtypes


def mxq(x, axis, fmt="e4m3"):
    dtype, down = {"e4m3": (ml_dtypes.float8_e4m3fn, 7), "e5m2": (ml_dtypes.float8_e5m2, 14)}[fmt]
    v = np.moveaxis(np.asarray(x, np.float32).astype(ml_dtypes.bfloat16).astype(np.float64), axis, -1)
    blocks = v.reshape(v.shape[:-1] + (-1, 32))
    amax = np.abs(blocks).max(-1, keepdims=True)
    byte = np.maximum(np.where(amax > 0, np.frexp(amax)[1] - 1 + 127, 0) - down, 1)
    scale = np.exp2(byte - 127.0)
    codes = (blocks / scale).astype(np.float32).astype(dtype).astype(np.float64)
    return np.moveaxis((codes * scale).reshape(v.shape), -1, axis)


WIDE = False


def mx_kscale(k):
    if not WIDE:
        return np.ones(k)
    levels = np.array([10, -10, 5, -5, 0])
    if k % 512:
        return np.exp2(np.random.permutation(np.resize(levels, k // 32))).repeat(32)
    a = np.empty((k // 512, 16))
    for p in range(k // 512):
        a[p, :8] = np.random.permutation(np.resize(levels, 8))
        for g in range(8):
            far = levels[np.abs(levels - a[p, g]) >= 10]
            a[p, g + 8] = far[np.random.randint(len(far))]
    return np.exp2(a.ravel()).repeat(32)


def f64(x):
    return np.asarray(x).astype(np.float64)


def striped8(idx):
    return np.asarray(idx).reshape(8, -1, 16).transpose(0, 2, 1).reshape(128, -1).astype(np.uint16)


def unstriped8(offs):
    return offs.reshape(8, 16, -1).transpose(0, 2, 1).reshape(8, -1).astype(np.int64)


def pick8(x, idx, run):
    r = np.arange(len(x))
    return x[r[:, None], idx[r % (8 * run) // run]]


E2M1 = np.array([0.0, 0.5, 1.0, 1.5, 2.0, 3.0, 4.0, 6.0, -0.0, -0.5, -1.0, -1.5, -2.0, -3.0, -4.0, -6.0])


def pack_weight(w, fmt):
    k, n = w.shape
    w = f64(np.asarray(w, np.float32).astype(ml_dtypes.bfloat16)).reshape(k // 32, 32, n)
    amax = np.abs(w).max(1)
    if fmt == "e4m3":
        byte = np.frexp(amax)[1] - 1 + 127 - 7
    else:
        mant, ex = np.frexp(amax / 6.0)
        byte = np.where(mant > 0.5, ex, ex - 1) + 127
    byte = np.clip(np.where(amax > 0, byte, 1), 1, 254)
    scaled = (w * np.exp2(127.0 - byte)[:, None, :]).reshape(k, n).astype(np.float32)
    by_word = np.ascontiguousarray(scaled.reshape(k // 512, 128, 4, n).transpose(0, 1, 3, 2))
    if fmt == "e4m3":
        words = by_word.astype(ml_dtypes.float8_e4m3fn).view(np.uint8)
    else:
        c = by_word.astype(ml_dtypes.float4_e2m1fn).view(np.uint8) & 0xF
        words = (c[..., 0::2] | (c[..., 1::2] << 4)).reshape(k // 512, 128, 2 * n)
    return np.ascontiguousarray(words), np.ascontiguousarray(byte.astype(np.uint8).reshape(k // 512, 16, n))


def unpack_weight(words, scales, fmt):
    g, _, n = scales.shape
    words = np.ascontiguousarray(words).reshape(g, 128, n, -1)
    if fmt == "e4m3":
        vals = words.view(ml_dtypes.float8_e4m3fn).astype(np.float64)
    else:
        nib = np.empty((g, 128, n, 4), np.uint8)
        nib[..., 0::2] = words & 0xF
        nib[..., 1::2] = words >> 4
        vals = E2M1[nib]
    vals = vals * np.repeat(np.exp2(scales.astype(np.float64) - 127.0), 8, axis=1)[..., None]
    return vals.transpose(0, 1, 3, 2).reshape(g * 512, n)


D, K, T, U, X, S, I, Q = 512, 512, 1024, 1024, 1024, 1024, 512, 128


def setup_inputs():
    n = np.random.standard_normal
    idx = np.stack([np.random.permutation(T)[:I] for _ in range(8)])
    idx2 = np.stack([np.random.permutation(U)[:I] for _ in range(8)])
    idx3 = np.stack([np.random.permutation(U)[:I] for _ in range(8)])
    idx4 = np.stack([np.random.permutation(X)[:I] for _ in range(8)])
    idx5 = np.stack([np.random.permutation(S)[:I] for _ in range(8)])
    idx6 = np.stack([np.random.permutation(S)[:I] for _ in range(8)])
    fd = mx_kscale(D)
    fk = mx_kscale(K)
    wqp = pack_weight(n((D, K)) * 1.0 / np.sqrt(D) * fd[:, None] * fk, "e4m3")
    keysp = pack_weight(n((K, T)) * 1.0 / np.sqrt(K) / fk[:, None], "e2m1")
    notesp = pack_weight(n((K, U)) * 1.0 / np.sqrt(K) / fk[:, None], "e4m3")
    usersp = pack_weight(n((D, X)) * 1.0 / np.sqrt(D) * fd[:, None], "e2m1")
    shelvesp = pack_weight(n((D, S)) * 1.0 / np.sqrt(D) * fd[:, None], "e4m3")
    return {
        "states": (n((D, Q)) * 0.95 / fd[:, None]).astype(np.float32),
        "wq_words": wqp[0],
        "wq_scales": wqp[1],
        "keys_words": keysp[0],
        "keys_scales": keysp[1],
        "notes_words": notesp[0],
        "notes_scales": notesp[1],
        "users_words": usersp[0],
        "users_scales": usersp[1],
        "shelves_words": shelvesp[0],
        "shelves_scales": shelvesp[1],
        "offs": striped8(idx),
        "offs2": striped8(idx2),
        "offs3": striped8(idx3),
        "offs4": striped8(idx4),
        "offs5": striped8(idx5),
        "offs6": striped8(idx6),
    }


def reference(states, wq_words, wq_scales, keys_words, keys_scales, notes_words, notes_scales, users_words, users_scales, shelves_words, shelves_scales, offs, offs2, offs3, offs4, offs5, offs6):
    idx = unstriped8(offs)
    idx2 = unstriped8(offs2)
    idx3 = unstriped8(offs3)
    idx4 = unstriped8(offs4)
    idx5 = unstriped8(offs5)
    idx6 = unstriped8(offs6)
    wqu = unpack_weight(wq_words, wq_scales, "e4m3")
    keysu = unpack_weight(keys_words, keys_scales, "e2m1")
    notesu = unpack_weight(notes_words, notes_scales, "e4m3")
    usersu = unpack_weight(users_words, users_scales, "e2m1")
    shelvesu = unpack_weight(shelves_words, shelves_scales, "e4m3")
    statesq = mxq(f64(states), 0, "e4m3")
    qv = wqu.T @ statesq
    qvq = mxq(qv, 0, "e4m3")
    a = qvq.T @ keysu
    b = qvq.T @ notesu
    c0 = statesq.T @ usersu
    d0 = statesq.T @ shelvesu
    f1 = np.zeros((Q, U))
    f1[np.arange(Q)[:, None], idx2[np.arange(Q) % 128 // 16]] = pick8(a, idx, 16)
    bb = b + f1
    w = np.maximum(pick8(bb, idx3, 16), pick8(c0, idx4, 16))
    f2 = np.zeros((Q, S))
    f2[np.arange(Q)[:, None], idx5[np.arange(Q) % 128 // 16]] = w
    dd = d0 - f2
    y = pick8(dd, idx6, 16) + pick8(c0, idx4, 16)
    return y

@@ -1,0 +1,187 @@
+from contextlib import ExitStack
+
+import concourse.mybir as mybir
+
+D, K, T, U, X, S, I, Q = 512, 512, 1024, 1024, 1024, 1024, 512, 128
+FLOPS = 2 * Q * (D * K + K * T + K * U + D * X + D * S)
+
+F32 = mybir.dt.float32
+BF16 = mybir.dt.bfloat16
+I32 = mybir.dt.int32
+U32 = mybir.dt.uint32
+U16 = mybir.dt.uint16
+U8 = mybir.dt.uint8
+FP8X4 = mybir.dt.float8_e4m3fn_x4
+FP4X4 = mybir.dt.float4_e2m1fn_x4
+ALU = mybir.AluOpType
+COPY = mybir.ActivationFunctionType.Copy
+
+P = 128
+PACK = 4
+BANK = 512
+QUARTER = 256
+HALF = I // 2
+HALF_COLS = HALF // 16
+
+
+def load_scale_rows(queue, plane, scales):
+    for quad in range(4):
+        queue.dma_start(
+            out=plane[32 * quad : 32 * quad + 4, :].bitcast(I32),
+            in_=scales[0, 4 * quad : 4 * quad + 4, :].bitcast(I32),
+        )
+
+
+def tile_attend_estuary_madefour_kernel(
+    tc, states, wq_words, wq_scales, keys_words, keys_scales, notes_words, notes_scales,
+    users_words, users_scales, shelves_words, shelves_scales,
+    offs, offs2, offs3, offs4, offs5, offs6, out,
+):
+    nc = tc.nc
+    with ExitStack() as ctx:
+        sb = ctx.enter_context(tc.tile_pool(name="sb", bufs=1))
+        ps = ctx.enter_context(tc.psum_pool(name="ps", bufs=1))
+
+        def load_list(src, name):
+            tile = sb.tile([P, I // 16], U16, name=name)
+            nc.sync.dma_start(tile[:], src)
+            return tile
+
+        def load_fp8(src, cols, name):
+            tile = sb.tile([P, cols], U32, name=name, align_bytes=64)
+            nc.sync.dma_start(out=tile[:].bitcast(I32), in_=src[0].rearrange("p n t -> p (n t)").bitcast(I32))
+            return tile
+
+        def load_fp4(src, cols, name):
+            tile = sb.tile([P, 2 * cols], U8, name=name, align_bytes=64)
+            nc.sync.dma_start(out=tile[:].bitcast(I32), in_=src[0].bitcast(I32))
+            return tile
+
+        wq_plane_raw = sb.tile([P, K], U8, align_bytes=64)
+        planes = sb.tile([P, X + T + U + S], U8, align_bytes=64)
+        nc.vector.memset(planes[:].bitcast(I32), 0)
+        users_plane = planes[:, 0:X]
+        keys_plane = planes[:, X : X + T]
+        notes_plane = planes[:, X + T : X + T + U]
+        shelves_plane = planes[:, X + T + U :]
+        f1 = sb.tile([P, U], F32)
+        nc.vector.memset(f1[:], 0.0)
+
+        states_raw = sb.tile([P, PACK, Q], F32)
+        nc.sync.dma_start(out=states_raw[:], in_=states.rearrange("(p j) q -> p j q", j=PACK))
+        for quad in range(4):
+            nc.sync.dma_start(
+                out=wq_plane_raw[32 * quad : 32 * quad + 32, :].bitcast(I32),
+                in_=wq_scales[0, 4 * quad : 4 * quad + 4, :].bitcast(I32).partition_broadcast(8),
+            )
+        wq_raw = load_fp8(wq_words, K, "wq_raw")
+        keys_w = load_fp4(keys_words, T, "keys_w")
+        load_scale_rows(nc.sync, keys_plane, keys_scales)
+        users_w = load_fp4(users_words, X, "users_w")
+        load_scale_rows(nc.sync, users_plane, users_scales)
+        list1 = load_list(offs, "list1")
+        list2 = load_list(offs2, "list2")
+        notes_w = load_fp8(notes_words, U, "notes_w")
+        load_scale_rows(nc.sync, notes_plane, notes_scales)
+        list4 = load_list(offs4, "list4")
+        list3 = load_list(offs3, "list3")
+        shelves_w = load_fp8(shelves_words, S, "shelves_w")
+        load_scale_rows(nc.sync, shelves_plane, shelves_scales)
+        list5 = load_list(offs5, "list5")
+        list6 = load_list(offs6, "list6")
+
+        states_bf = sb.tile([P, Q, PACK], BF16, align_bytes=64, tag="states_bf_then_f2")
+        nc.vector.tensor_copy(out=states_bf[:], in_=states_raw[:].rearrange("p j q -> p q j"))
+        wq_plane = sb.tile([P, K], U8, align_bytes=64)
+        nc.vector.tensor_copy(
+            out=wq_plane[:].rearrange("p (t m) -> p m t", t=PACK),
+            in_=wq_plane_raw[:].rearrange("p (m t) -> p m t", t=PACK),
+        )
+        st_codes = sb.tile([P, Q], U32, align_bytes=64)
+        st_plane = sb.tile([P, Q], U8, align_bytes=64)
+        nc.vector.quantize_mx(
+            out=st_codes[:].bitcast(FP8X4), scales=st_plane[:], in_=states_bf[:].rearrange("p q j -> p (q j)")
+        )
+        wq_dealt = sb.tile([P, K], U32, align_bytes=64)
+        nc.scalar.copy(
+            out=wq_dealt[:].rearrange("p (t m) -> p m t", t=PACK),
+            in_=wq_raw[:].rearrange("p (m t) -> p m t", t=PACK),
+        )
+
+        qv_ps = ps.tile([P, PACK, Q], F32, tag="bank_qv")
+        for t in range(PACK):
+            cols = slice(t * P, (t + 1) * P)
+            nc.tensor.matmul_mx(
+                out=qv_ps[:, t, :], lhsT=wq_dealt[:, cols].bitcast(FP8X4), lhsT_scale=wq_plane[:, cols],
+                rhs=st_codes[:].bitcast(FP8X4), rhs_scale=st_plane[:], start=True, stop=True,
+            )
+        qv_bf = sb.tile([P, Q, PACK], BF16, align_bytes=64)
+        nc.vector.tensor_copy(out=qv_bf[:], in_=qv_ps[:].rearrange("p t q -> p q t"))
+        qv_codes = sb.tile([P, Q], U32, align_bytes=64)
+        qv_plane = sb.tile([P, Q], U8, align_bytes=64)
+        nc.vector.quantize_mx(
+            out=qv_codes[:].bitcast(FP8X4), scales=qv_plane[:], in_=qv_bf[:].rearrange("p q j -> p (q j)")
+        )
+        f2 = sb.tile([P, S], F32, align_bytes=64, tag="states_bf_then_f2")
+        nc.vector.memset(f2[:], 0.0)
+
+        def score(codes, plane, words, words_plane, c0, n, is_fp4, tag):
+            bank = ps.tile([P, n], F32, tag=tag, name=tag)
+            rhs = words[:, 2 * c0 : 2 * (c0 + n)].bitcast(FP4X4) if is_fp4 else words[:, c0 : c0 + n].bitcast(FP8X4)
+            nc.tensor.matmul_mx(
+                out=bank[:], lhsT=codes[:].bitcast(FP8X4), lhsT_scale=plane[:],
+                rhs=rhs, rhs_scale=words_plane[:, c0 : c0 + n], start=True, stop=True,
+            )
+            return bank
+
+        a_sb = sb.tile([P, T], F32, tag="a_then_c0")
+        for j in range(T // QUARTER):
+            bank = score(qv_codes, qv_plane, keys_w, keys_plane, j * QUARTER, QUARTER, True, "bank_a%d" % j)
+            dst = a_sb[:, j * QUARTER : (j + 1) * QUARTER]
+            if j % 2 == 0:
+                nc.scalar.activation(dst, bank[:], COPY)
+            else:
+                nc.vector.tensor_copy(dst, bank[:])
+        c_banks = [score(st_codes, st_plane, users_w, users_plane, h * BANK, BANK, True, "bank_c%d" % h) for h in range(2)]
+        b_banks = [
+            score(qv_codes, qv_plane, notes_w, notes_plane, h * BANK, BANK, False, tag)
+            for h, tag in enumerate(("bank_b0", "bank_qv"))
+        ]
+        d_banks = [
+            score(st_codes, st_plane, shelves_w, shelves_plane, h * BANK, BANK, False, "bank_a%d" % h) for h in range(2)
+        ]
+
+        a_picked = sb.tile([P, I], F32)
+        nc.vector.tensor_copy(a_picked[:, :HALF], a_sb[:].indirect(list1[:, :HALF_COLS]))
+        nc.scalar.activation(a_picked[:, HALF:], a_sb[:].indirect(list1[:, HALF_COLS:]), COPY)
+        nc.vector.tensor_copy(f1[:].indirect(list2[:]), a_picked[:])
+
+        c_sb = sb.tile([P, X], F32, tag="a_then_c0")
+        for h in range(2):
+            nc.scalar.activation(c_sb[:, h * BANK : (h + 1) * BANK], c_banks[h][:], COPY)
+        c_picked = sb.tile([P, I], F32)
+        nc.scalar.activation(c_picked[:], c_sb[:].indirect(list4[:]), COPY)
+
+        bb = sb.tile([P, U], F32)
+        for h in range(2):
+            cols = slice(h * BANK, (h + 1) * BANK)
+            nc.vector.tensor_tensor(bb[:, cols], b_banks[h][:], f1[:, cols], ALU.add)
+        bb_picked = sb.tile([P, I], F32)
+        nc.vector.tensor_copy(bb_picked[:, :HALF], bb[:].indirect(list3[:, :HALF_COLS]))
+        nc.scalar.activation(bb_picked[:, HALF:], bb[:].indirect(list3[:, HALF_COLS:]), COPY)
+        w = sb.tile([P, I], F32)
+        nc.vector.tensor_tensor(w[:], bb_picked[:], c_picked[:], ALU.max)
+        nc.vector.tensor_copy(f2[:].indirect(list5[:]), w[:])
+
+        dd = sb.tile([P, S], F32)
+        for h in range(2):
+            cols = slice(h * BANK, (h + 1) * BANK)
+            nc.vector.tensor_tensor(dd[:, cols], d_banks[h][:], f2[:, cols], ALU.subtract)
+        y_lo = sb.tile([P, HALF], F32)
+        nc.vector.tensor_tensor(y_lo[:], dd[:].indirect(list6[:, :HALF_COLS]), c_picked[:, :HALF], ALU.add)
+        nc.sync.dma_start(out=out[:, :HALF], in_=y_lo[:])
+        dd_picked = sb.tile([P, HALF], F32)
+        nc.scalar.activation(dd_picked[:], dd[:].indirect(list6[:, HALF_COLS:]), COPY)
+        y_hi = sb.tile([P, HALF], F32)
+        nc.vector.tensor_tensor(y_hi[:], dd_picked[:], c_picked[:, HALF:], ALU.add)
+        nc.scalar.dma_start(out=out[:, HALF:], in_=y_hi[:])

@@ -22,6 +22,7 @@ BANK = 512
 QUARTER = 256
 HALF = I // 2
 HALF_COLS = HALF // 16
+VEC_COLS = 768
 
 
 def load_scale_rows(queue, plane, scales):
@@ -66,6 +67,8 @@ def tile_attend_estuary_madefour_kernel(
         shelves_plane = planes[:, X + T + U :]
         f1 = sb.tile([P, U], F32)
         nc.vector.memset(f1[:], 0.0)
+        f2 = sb.tile([P, S], F32)
+        nc.gpsimd.memset(f2[:], 0.0)
 
         states_raw = sb.tile([P, PACK, Q], F32)
         nc.sync.dma_start(out=states_raw[:], in_=states.rearrange("(p j) q -> p j q", j=PACK))
@@ -75,10 +78,10 @@ def tile_attend_estuary_madefour_kernel(
                 in_=wq_scales[0, 4 * quad : 4 * quad + 4, :].bitcast(I32).partition_broadcast(8),
             )
         wq_raw = load_fp8(wq_words, K, "wq_raw")
-        keys_w = load_fp4(keys_words, T, "keys_w")
-        load_scale_rows(nc.sync, keys_plane, keys_scales)
         users_w = load_fp4(users_words, X, "users_w")
         load_scale_rows(nc.sync, users_plane, users_scales)
+        keys_w = load_fp4(keys_words, T, "keys_w")
+        load_scale_rows(nc.sync, keys_plane, keys_scales)
         list1 = load_list(offs, "list1")
         list2 = load_list(offs2, "list2")
         notes_w = load_fp8(notes_words, U, "notes_w")
@@ -90,29 +93,32 @@ def tile_attend_estuary_madefour_kernel(
         list5 = load_list(offs5, "list5")
         list6 = load_list(offs6, "list6")
 
-        states_bf = sb.tile([P, Q, PACK], BF16, align_bytes=64, tag="states_bf_then_f2")
-        nc.vector.tensor_copy(out=states_bf[:], in_=states_raw[:].rearrange("p j q -> p q j"))
-        wq_plane = sb.tile([P, K], U8, align_bytes=64)
+        states_bf = sb.tile([P, Q, PACK], BF16, align_bytes=64)
         nc.vector.tensor_copy(
-            out=wq_plane[:].rearrange("p (t m) -> p m t", t=PACK),
-            in_=wq_plane_raw[:].rearrange("p (m t) -> p m t", t=PACK),
+            out=states_bf[:].rearrange("p (c i) j -> p c j i", i=4),
+            in_=states_raw[:].rearrange("p j (c i) -> p c j i", i=4),
         )
         st_codes = sb.tile([P, Q], U32, align_bytes=64)
         st_plane = sb.tile([P, Q], U8, align_bytes=64)
         nc.vector.quantize_mx(
             out=st_codes[:].bitcast(FP8X4), scales=st_plane[:], in_=states_bf[:].rearrange("p q j -> p (q j)")
         )
-        wq_dealt = sb.tile([P, K], U32, align_bytes=64)
-        nc.scalar.copy(
-            out=wq_dealt[:].rearrange("p (t m) -> p m t", t=PACK),
-            in_=wq_raw[:].rearrange("p (m t) -> p m t", t=PACK),
-        )
+        words_by_place = wq_raw[:].rearrange("p (m t) -> p m t", t=PACK)
+        bytes_by_place = wq_plane_raw[:].rearrange("p (m t) -> p t m", t=PACK)
+        wq_dealt, wq_plane = [], []
+        for h in range(2):
+            places = slice(2 * h, 2 * h + 2)
+            words = sb.tile([P, 2, P], U32, align_bytes=64, name="wq_dealt%d" % h)
+            nc.scalar.copy(out=words[:].rearrange("p t m -> p m t"), in_=words_by_place[:, :, places])
+            plane = sb.tile([P, 2, P], U8, align_bytes=64, name="wq_plane%d" % h)
+            nc.vector.tensor_copy(out=plane[:], in_=bytes_by_place[:, places, :])
+            wq_dealt.append(words)
+            wq_plane.append(plane)
 
         qv_ps = ps.tile([P, PACK, Q], F32, tag="bank_qv")
         for t in range(PACK):
-            cols = slice(t * P, (t + 1) * P)
             nc.tensor.matmul_mx(
-                out=qv_ps[:, t, :], lhsT=wq_dealt[:, cols].bitcast(FP8X4), lhsT_scale=wq_plane[:, cols],
+                out=qv_ps[:, t, :], lhsT=wq_dealt[t // 2][:, t % 2, :].bitcast(FP8X4), lhsT_scale=wq_plane[t // 2][:, t % 2, :],
                 rhs=st_codes[:].bitcast(FP8X4), rhs_scale=st_plane[:], start=True, stop=True,
             )
         qv_bf = sb.tile([P, Q, PACK], BF16, align_bytes=64)
@@ -122,8 +128,6 @@ def tile_attend_estuary_madefour_kernel(
         nc.vector.quantize_mx(
             out=qv_codes[:].bitcast(FP8X4), scales=qv_plane[:], in_=qv_bf[:].rearrange("p q j -> p (q j)")
         )
-        f2 = sb.tile([P, S], F32, align_bytes=64, tag="states_bf_then_f2")
-        nc.vector.memset(f2[:], 0.0)
 
         def score(codes, plane, words, words_plane, c0, n, is_fp4, tag):
             bank = ps.tile([P, n], F32, tag=tag, name=tag)
@@ -162,21 +166,28 @@ def tile_attend_estuary_madefour_kernel(
         c_picked = sb.tile([P, I], F32)
         nc.scalar.activation(c_picked[:], c_sb[:].indirect(list4[:]), COPY)
 
-        bb = sb.tile([P, U], F32)
-        for h in range(2):
-            cols = slice(h * BANK, (h + 1) * BANK)
-            nc.vector.tensor_tensor(bb[:, cols], b_banks[h][:], f1[:, cols], ALU.add)
+        def combine(banks, scattered, op, name):
+            tail = sb.tile([P, 2 * BANK - VEC_COLS], F32, name=name + "_tail")
+            nc.scalar.activation(tail[:], banks[1][:, VEC_COLS - BANK :], COPY)
+            result = sb.tile([P, 2 * BANK], F32, name=name)
+            nc.gpsimd.tensor_tensor(result[:, VEC_COLS:], tail[:], scattered[:, VEC_COLS:], op)
+            nc.vector.tensor_tensor(result[:, :BANK], banks[0][:], scattered[:, :BANK], op)
+            nc.vector.tensor_tensor(
+                result[:, BANK:VEC_COLS], banks[1][:, : VEC_COLS - BANK], scattered[:, BANK:VEC_COLS], op
+            )
+            return result
+
+        bb = combine(b_banks, f1, ALU.add, "bb")
         bb_picked = sb.tile([P, I], F32)
         nc.vector.tensor_copy(bb_picked[:, :HALF], bb[:].indirect(list3[:, :HALF_COLS]))
         nc.scalar.activation(bb_picked[:, HALF:], bb[:].indirect(list3[:, HALF_COLS:]), COPY)
         w = sb.tile([P, I], F32)
-        nc.vector.tensor_tensor(w[:], bb_picked[:], c_picked[:], ALU.max)
+        for h in range(2):
+            cols = slice(h * HALF, (h + 1) * HALF)
+            nc.vector.tensor_tensor(w[:, cols], bb_picked[:, cols], c_picked[:, cols], ALU.max)
         nc.vector.tensor_copy(f2[:].indirect(list5[:]), w[:])
 
-        dd = sb.tile([P, S], F32)
-        for h in range(2):
-            cols = slice(h * BANK, (h + 1) * BANK)
-            nc.vector.tensor_tensor(dd[:, cols], d_banks[h][:], f2[:, cols], ALU.subtract)
+        dd = combine(d_banks, f2, ALU.subtract, "dd")
         y_lo = sb.tile([P, HALF], F32)
         nc.vector.tensor_tensor(y_lo[:], dd[:].indirect(list6[:, :HALF_COLS]), c_picked[:, :HALF], ALU.add)
         nc.sync.dma_start(out=out[:, :HALF], in_=y_lo[:])

@@ -115,14 +115,19 @@ def tile_attend_estuary_madefour_kernel(
             wq_dealt.append(words)
             wq_plane.append(plane)
 
-        qv_ps = ps.tile([P, PACK, Q], F32, tag="bank_qv")
-        for t in range(PACK):
-            nc.tensor.matmul_mx(
-                out=qv_ps[:, t, :], lhsT=wq_dealt[t // 2][:, t % 2, :].bitcast(FP8X4), lhsT_scale=wq_plane[t // 2][:, t % 2, :],
-                rhs=st_codes[:].bitcast(FP8X4), rhs_scale=st_plane[:], start=True, stop=True,
-            )
         qv_bf = sb.tile([P, Q, PACK], BF16, align_bytes=64)
-        nc.vector.tensor_copy(out=qv_bf[:], in_=qv_ps[:].rearrange("p t q -> p q t"))
+        for h in range(2):
+            qv_ps = ps.tile([P, 2, Q], F32, tag="bank_qv%d" % h, name="qv_ps%d" % h)
+            for t in range(2):
+                nc.tensor.matmul_mx(
+                    out=qv_ps[:, t, :], lhsT=wq_dealt[h][:, t, :].bitcast(FP8X4), lhsT_scale=wq_plane[h][:, t, :],
+                    rhs=st_codes[:].bitcast(FP8X4), rhs_scale=st_plane[:], start=True, stop=True,
+                )
+            pair = qv_bf[:, :, 2 * h : 2 * h + 2]
+            if h == 0:
+                nc.vector.tensor_copy(out=pair, in_=qv_ps[:].rearrange("p t q -> p q t"))
+            else:
+                nc.scalar.copy(out=pair, in_=qv_ps[:].rearrange("p t q -> p q t"))
         qv_codes = sb.tile([P, Q], U32, align_bytes=64)
         qv_plane = sb.tile([P, Q], U8, align_bytes=64)
         nc.vector.quantize_mx(
@@ -149,7 +154,7 @@ def tile_attend_estuary_madefour_kernel(
         c_banks = [score(st_codes, st_plane, users_w, users_plane, h * BANK, BANK, True, "bank_c%d" % h) for h in range(2)]
         b_banks = [
             score(qv_codes, qv_plane, notes_w, notes_plane, h * BANK, BANK, False, tag)
-            for h, tag in enumerate(("bank_b0", "bank_qv"))
+            for h, tag in enumerate(("bank_qv0", "bank_qv1"))
         ]
         d_banks = [
             score(st_codes, st_plane, shelves_w, shelves_plane, h * BANK, BANK, False, "bank_a%d" % h) for h in range(2)

from contextlib import ExitStack

import concourse.mybir as mybir

D, K, T, U, X, S, I, Q = 512, 512, 1024, 1024, 1024, 1024, 512, 128
FLOPS = 2 * Q * (D * K + K * T + K * U + D * X + D * S)

F32 = mybir.dt.float32
BF16 = mybir.dt.bfloat16
I32 = mybir.dt.int32
U32 = mybir.dt.uint32
U16 = mybir.dt.uint16
U8 = mybir.dt.uint8
FP8X4 = mybir.dt.float8_e4m3fn_x4
FP4X4 = mybir.dt.float4_e2m1fn_x4
ALU = mybir.AluOpType
COPY = mybir.ActivationFunctionType.Copy

P = 128
PACK = 4
BANK = 512
QUARTER = 256
HALF = I // 2
HALF_COLS = HALF // 16
VEC_COLS = 768


def load_scale_rows(queue, plane, scales):
    for quad in range(4):
        queue.dma_start(
            out=plane[32 * quad : 32 * quad + 4, :].bitcast(I32),
            in_=scales[0, 4 * quad : 4 * quad + 4, :].bitcast(I32),
        )


def tile_attend_estuary_madefour_kernel(
    tc, states, wq_words, wq_scales, keys_words, keys_scales, notes_words, notes_scales,
    users_words, users_scales, shelves_words, shelves_scales,
    offs, offs2, offs3, offs4, offs5, offs6, out,
):
    nc = tc.nc
    with ExitStack() as ctx:
        sb = ctx.enter_context(tc.tile_pool(name="sb", bufs=1))
        ps = ctx.enter_context(tc.psum_pool(name="ps", bufs=1))

        def load_list(src, name):
            tile = sb.tile([P, I // 16], U16, name=name)
            nc.sync.dma_start(tile[:], src)
            return tile

        def load_fp8(src, cols, name):
            tile = sb.tile([P, cols], U32, name=name, align_bytes=64)
            nc.sync.dma_start(out=tile[:].bitcast(I32), in_=src[0].rearrange("p n t -> p (n t)").bitcast(I32))
            return tile

        def load_fp4(src, cols, name):
            tile = sb.tile([P, 2 * cols], U8, name=name, align_bytes=64)
            nc.sync.dma_start(out=tile[:].bitcast(I32), in_=src[0].bitcast(I32))
            return tile

        wq_plane_raw = sb.tile([P, K], U8, align_bytes=64)
        planes = sb.tile([P, X + T + U + S], U8, align_bytes=64)
        nc.vector.memset(planes[:].bitcast(I32), 0)
        users_plane = planes[:, 0:X]
        keys_plane = planes[:, X : X + T]
        notes_plane = planes[:, X + T : X + T + U]
        shelves_plane = planes[:, X + T + U :]
        f1 = sb.tile([P, U], F32)
        nc.vector.memset(f1[:], 0.0)
        f2 = sb.tile([P, S], F32)
        nc.gpsimd.memset(f2[:], 0.0)

        states_raw = sb.tile([P, PACK, Q], F32)
        nc.sync.dma_start(out=states_raw[:], in_=states.rearrange("(p j) q -> p j q", j=PACK))
        for quad in range(4):
            nc.sync.dma_start(
                out=wq_plane_raw[32 * quad : 32 * quad + 32, :].bitcast(I32),
                in_=wq_scales[0, 4 * quad : 4 * quad + 4, :].bitcast(I32).partition_broadcast(8),
            )
        wq_raw = load_fp8(wq_words, K, "wq_raw")
        users_w = load_fp4(users_words, X, "users_w")
        load_scale_rows(nc.sync, users_plane, users_scales)
        keys_w = load_fp4(keys_words, T, "keys_w")
        load_scale_rows(nc.sync, keys_plane, keys_scales)
        list1 = load_list(offs, "list1")
        list2 = load_list(offs2, "list2")
        notes_w = load_fp8(notes_words, U, "notes_w")
        load_scale_rows(nc.sync, notes_plane, notes_scales)
        list4 = load_list(offs4, "list4")
        list3 = load_list(offs3, "list3")
        shelves_w = load_fp8(shelves_words, S, "shelves_w")
        load_scale_rows(nc.sync, shelves_plane, shelves_scales)
        list5 = load_list(offs5, "list5")
        list6 = load_list(offs6, "list6")

        states_bf = sb.tile([P, Q, PACK], BF16, align_bytes=64)
        nc.vector.tensor_copy(
            out=states_bf[:].rearrange("p (c i) j -> p c j i", i=4),
            in_=states_raw[:].rearrange("p j (c i) -> p c j i", i=4),
        )
        st_codes = sb.tile([P, Q], U32, align_bytes=64)
        st_plane = sb.tile([P, Q], U8, align_bytes=64)
        nc.vector.quantize_mx(
            out=st_codes[:].bitcast(FP8X4), scales=st_plane[:], in_=states_bf[:].rearrange("p q j -> p (q j)")
        )
        words_by_place = wq_raw[:].rearrange("p (m t) -> p m t", t=PACK)
        bytes_by_place = wq_plane_raw[:].rearrange("p (m t) -> p t m", t=PACK)
        wq_dealt, wq_plane = [], []
        for h in range(2):
            places = slice(2 * h, 2 * h + 2)
            words = sb.tile([P, 2, P], U32, align_bytes=64, name="wq_dealt%d" % h)
            nc.scalar.copy(out=words[:].rearrange("p t m -> p m t"), in_=words_by_place[:, :, places])
            plane = sb.tile([P, 2, P], U8, align_bytes=64, name="wq_plane%d" % h)
            nc.vector.tensor_copy(out=plane[:], in_=bytes_by_place[:, places, :])
            wq_dealt.append(words)
            wq_plane.append(plane)

        qv_bf = sb.tile([P, Q, PACK], BF16, align_bytes=64)
        for h in range(2):
            qv_ps = ps.tile([P, 2, Q], F32, tag="bank_qv%d" % h, name="qv_ps%d" % h)
            for t in range(2):
                nc.tensor.matmul_mx(
                    out=qv_ps[:, t, :], lhsT=wq_dealt[h][:, t, :].bitcast(FP8X4), lhsT_scale=wq_plane[h][:, t, :],
                    rhs=st_codes[:].bitcast(FP8X4), rhs_scale=st_plane[:], start=True, stop=True,
                )
            pair = qv_bf[:, :, 2 * h : 2 * h + 2]
            if h == 0:
                nc.vector.tensor_copy(out=pair, in_=qv_ps[:].rearrange("p t q -> p q t"))
            else:
                nc.scalar.copy(out=pair, in_=qv_ps[:].rearrange("p t q -> p q t"))
        qv_codes = sb.tile([P, Q], U32, align_bytes=64)
        qv_plane = sb.tile([P, Q], U8, align_bytes=64)
        nc.vector.quantize_mx(
            out=qv_codes[:].bitcast(FP8X4), scales=qv_plane[:], in_=qv_bf[:].rearrange("p q j -> p (q j)")
        )

        def score(codes, plane, words, words_plane, c0, n, is_fp4, tag):
            bank = ps.tile([P, n], F32, tag=tag, name=tag)
            rhs = words[:, 2 * c0 : 2 * (c0 + n)].bitcast(FP4X4) if is_fp4 else words[:, c0 : c0 + n].bitcast(FP8X4)
            nc.tensor.matmul_mx(
                out=bank[:], lhsT=codes[:].bitcast(FP8X4), lhsT_scale=plane[:],
                rhs=rhs, rhs_scale=words_plane[:, c0 : c0 + n], start=True, stop=True,
            )
            return bank

        a_sb = sb.tile([P, T], F32, tag="a_then_c0")
        for j in range(T // QUARTER):
            bank = score(qv_codes, qv_plane, keys_w, keys_plane, j * QUARTER, QUARTER, True, "bank_a%d" % j)
            dst = a_sb[:, j * QUARTER : (j + 1) * QUARTER]
            if j % 2 == 0:
                nc.scalar.activation(dst, bank[:], COPY)
            else:
                nc.vector.tensor_copy(dst, bank[:])
        c_banks = [score(st_codes, st_plane, users_w, users_plane, h * BANK, BANK, True, "bank_c%d" % h) for h in range(2)]
        b_banks = [
            score(qv_codes, qv_plane, notes_w, notes_plane, h * BANK, BANK, False, tag)
            for h, tag in enumerate(("bank_qv0", "bank_qv1"))
        ]
        d_banks = [
            score(st_codes, st_plane, shelves_w, shelves_plane, h * BANK, BANK, False, "bank_a%d" % h) for h in range(2)
        ]

        a_picked = sb.tile([P, I], F32)
        nc.vector.tensor_copy(a_picked[:, :HALF], a_sb[:].indirect(list1[:, :HALF_COLS]))
        nc.scalar.activation(a_picked[:, HALF:], a_sb[:].indirect(list1[:, HALF_COLS:]), COPY)
        nc.vector.tensor_copy(f1[:].indirect(list2[:]), a_picked[:])

        c_sb = sb.tile([P, X], F32, tag="a_then_c0")
        for h in range(2):
            nc.scalar.activation(c_sb[:, h * BANK : (h + 1) * BANK], c_banks[h][:], COPY)
        c_picked = sb.tile([P, I], F32)
        nc.scalar.activation(c_picked[:], c_sb[:].indirect(list4[:]), COPY)

        def combine(banks, scattered, op, name):
            tail = sb.tile([P, 2 * BANK - VEC_COLS], F32, name=name + "_tail")
            nc.scalar.activation(tail[:], banks[1][:, VEC_COLS - BANK :], COPY)
            result = sb.tile([P, 2 * BANK], F32, name=name)
            nc.gpsimd.tensor_tensor(result[:, VEC_COLS:], tail[:], scattered[:, VEC_COLS:], op)
            nc.vector.tensor_tensor(result[:, :BANK], banks[0][:], scattered[:, :BANK], op)
            nc.vector.tensor_tensor(
                result[:, BANK:VEC_COLS], banks[1][:, : VEC_COLS - BANK], scattered[:, BANK:VEC_COLS], op
            )
            return result

        bb = combine(b_banks, f1, ALU.add, "bb")
        bb_picked = sb.tile([P, I], F32)
        nc.vector.tensor_copy(bb_picked[:, :HALF], bb[:].indirect(list3[:, :HALF_COLS]))
        nc.scalar.activation(bb_picked[:, HALF:], bb[:].indirect(list3[:, HALF_COLS:]), COPY)
        w = sb.tile([P, I], F32)
        for h in range(2):
            cols = slice(h * HALF, (h + 1) * HALF)
            nc.vector.tensor_tensor(w[:, cols], bb_picked[:, cols], c_picked[:, cols], ALU.max)
        nc.vector.tensor_copy(f2[:].indirect(list5[:]), w[:])

        dd = combine(d_banks, f2, ALU.subtract, "dd")
        y_lo = sb.tile([P, HALF], F32)
        nc.vector.tensor_tensor(y_lo[:], dd[:].indirect(list6[:, :HALF_COLS]), c_picked[:, :HALF], ALU.add)
        nc.sync.dma_start(out=out[:, :HALF], in_=y_lo[:])
        dd_picked = sb.tile([P, HALF], F32)
        nc.scalar.activation(dd_picked[:], dd[:].indirect(list6[:, HALF_COLS:]), COPY)
        y_hi = sb.tile([P, HALF], F32)
        nc.vector.tensor_tensor(y_hi[:], dd_picked[:], c_picked[:, HALF:], ALU.add)
        nc.scalar.dma_start(out=out[:, HALF:], in_=y_hi[:])
